import numpy as np
import ml_dtypes


def mxq(x, axis, fmt="e4m3"):
    dtype, down = {"e4m3": (ml_dtypes.float8_e4m3fn, 7), "e5m2": (ml_dtypes.float8_e5m2, 14)}[fmt]
    v = np.moveaxis(np.asarray(x, np.float32).astype(ml_dtypes.bfloat16).astype(np.float64), axis, -1)
    blocks = v.reshape(v.shape[:-1] + (-1, 32))
    amax = np.abs(blocks).max(-1, keepdims=True)
    byte = np.maximum(np.where(amax > 0, np.frexp(amax)[1] - 1 + 127, 0) - down, 1)
    scale = np.exp2(byte - 127.0)
    codes = (blocks / scale).astype(np.float32).astype(dtype).astype(np.float64)
    return np.moveaxis((codes * scale).reshape(v.shape), -1, axis)


WIDE = False


def mx_kscale(k, group=512):
    if not WIDE:
        return np.ones(k)
    levels = np.array([18, -18])
    if group != 512:
        return np.exp2(np.random.permutation(np.resize(levels, k // group))).repeat(group)
    if k % 512:
        return np.exp2(np.random.permutation(np.resize(levels, k // 32))).repeat(32)
    a = np.empty((k // 512, 16))
    for p in range(k // 512):
        a[p, :8] = np.random.permutation(np.resize(levels, 8))
        for g in range(8):
            far = levels[np.abs(levels - a[p, g]) >= 10]
            a[p, g + 8] = far[np.random.randint(len(far))]
    return np.exp2(a.ravel()).repeat(32)


def f64(x):
    return np.asarray(x).astype(np.float64)


G, D, M, N = 4, 128, 256, 512


def setup_inputs():
    n = np.random.standard_normal
    s_d = mx_kscale(D, 0)
    return {
        "x": (n((G, D, M)) / s_d[:, None] / np.sqrt(D)).astype(np.float32),
        "c": (n((G, D, N)) * s_d[:, None]).astype(np.float32),
        "u": (np.where(np.arange(N)[None, None] == np.random.randint(0, N, (G, M, 1)), 1.0, 0.0)).astype(np.float32),
    }


def reference(x, c, u):
    xq = mxq(f64(x), 1, "e4m3")
    cq = mxq(f64(c), 1, "e4m3")
    z = xq.transpose(0, 2, 1) @ cq
    rt = np.sum(z * f64(u), axis=-1, keepdims=True)
    y = np.maximum(z + 1.0 - rt - f64(u), 0.0)
    return y

@@ -1,0 +1,154 @@
+from contextlib import ExitStack
+
+import concourse.mybir as mybir
+
+G, D, M, N = 4, 128, 256, 512
+FLOPS = 2 * G * D * M * N
+
+F32 = mybir.dt.float32
+BF16 = mybir.dt.bfloat16
+U32 = mybir.dt.uint32
+U8 = mybir.dt.uint8
+FP8X4 = mybir.dt.float8_e4m3fn_x4
+ALU = mybir.AluOpType
+ACT = mybir.ActivationFunctionType
+
+P = 128
+PACK = 4
+ROWS = D // PACK
+HALVES = M // P
+NQ = 128
+C_LOAD = 256
+
+
+def interleave(copy, grouped, raw, lo, hi, base):
+    copy(
+        out=grouped[:, base + lo : base + hi, :].rearrange("p (c i) j -> p c j i", i=4),
+        in_=raw[:, :, lo:hi].rearrange("p j (c i) -> p c j i", i=4),
+    )
+
+
+def tile_rows_hinge_kernel(tc, x, c, u, out):
+    nc = tc.nc
+    with ExitStack() as ctx:
+        sb = ctx.enter_context(tc.tile_pool(name="sb", bufs=1))
+        ps = ctx.enter_context(tc.psum_pool(name="ps", bufs=1))
+        ctx.enter_context(tc.manual_schedule())
+
+        x_raw = sb.tile([P, PACK, M], F32, name="x_raw")
+        c_raw = [sb.tile([P, PACK, C_LOAD], F32, name="c_raw%d" % h) for h in range(N // C_LOAD)]
+        u_sb = [sb.tile([P, HALVES, N], F32, name="u%d" % g) for g in range(G)]
+        y_sb = [sb.tile([P, HALVES, N], F32, name="y%d" % g) for g in range(G)]
+        diff = [sb.tile([P, HALVES, N], F32, name="diff%d" % g) for g in range(G)]
+        prod = [sb.tile([P, HALVES, N], F32, name="prod%d" % g) for g in range(G)]
+        z1 = [sb.tile([P, N], F32, name="z1_%d" % g) for g in range(G)]
+        neg_rt = sb.tile([P, G * HALVES], F32, name="neg_rt")
+        x_bf = sb.tile([P, HALVES, P, PACK], BF16, name="x_bf", align_bytes=64)
+        c_bf = sb.tile([P, N, PACK], BF16, name="c_bf", align_bytes=64)
+        x_codes = sb.tile([P, M], U32, name="x_codes", align_bytes=64)
+        x_scales = sb.tile([P, M], U8, name="x_scales", align_bytes=64)
+        c_codes = sb.tile([P, N], U32, name="c_codes", align_bytes=64)
+        c_scales = sb.tile([P, N], U8, name="c_scales", align_bytes=64)
+        z = [[ps.tile([P, N], F32, name="z%d_%d" % (g, t)) for t in range(HALVES)] for g in range(G)]
+
+        x_view = x.rearrange("g (p j) m -> (g p) j m", j=PACK)
+        c_view = c.rearrange("g (p j) n -> (g p) j n", j=PACK)
+        u_view = u.rearrange("g (s t) n -> g s t n", t=HALVES)
+        out_view = out.rearrange("g (s t) n -> g s t n", t=HALVES)
+
+        nc.sync.dma_start(out=x_raw[:], in_=x_view)
+        for h in range(N // C_LOAD):
+            nc.sync.dma_start(out=c_raw[h][:], in_=c_view[:, :, h * C_LOAD : (h + 1) * C_LOAD])
+        for g in range(G):
+            nc.sync.dma_start(out=u_sb[g][:], in_=u_view[g])
+
+        def quantize(codes, scales, grouped, lo, hi):
+            nc.vector.quantize_mx(
+                out=codes[:, lo:hi].bitcast(FP8X4),
+                scales=scales[:, lo:hi],
+                in_=grouped[:, lo:hi, :].rearrange("p n j -> p (n j)"),
+            )
+
+        def score(g, t, q):
+            rows = slice(g * ROWS, (g + 1) * ROWS)
+            ms = slice(t * P, (t + 1) * P)
+            ns = slice(q * NQ, (q + 1) * NQ)
+            nc.tensor.matmul_mx(
+                out=z[g][t][:, ns],
+                lhsT=x_codes[rows, ms].bitcast(FP8X4),
+                lhsT_scale=x_scales[rows, ms],
+                rhs=c_codes[rows, ns].bitcast(FP8X4),
+                rhs_scale=c_scales[rows, ns],
+                start=True,
+                stop=True,
+            )
+
+        x_dealt = x_raw[:].rearrange("p j (s t) -> p t s j", t=HALVES)
+        nc.scalar.activation(out=x_bf[:, 1], in_=x_dealt[:, 1], func=ACT.Copy)
+        nc.vector.tensor_copy(out=x_bf[:, 0], in_=x_dealt[:, 0])
+        quantize(x_codes, x_scales, x_bf[:].rearrange("p t s j -> p (t s) j"), 0, M)
+
+        interleave(nc.vector.tensor_copy, c_bf, c_raw[0], 0, 160, 0)
+        interleave(nc.scalar.copy, c_bf, c_raw[0], 160, 256, 0)
+        quantize(c_codes, c_scales, c_bf, 0, 256)
+        early = [(0, 0), (0, 1), (1, 1)]
+        for g, t in early:
+            for q in range(2):
+                score(g, t, q)
+
+        interleave(nc.vector.tensor_copy, c_bf, c_raw[1], 0, 128, 256)
+        interleave(nc.scalar.copy, c_bf, c_raw[1], 128, 224, 256)
+        interleave(nc.vector.tensor_copy, c_bf, c_raw[1], 224, 256, 256)
+        quantize(c_codes, c_scales, c_bf, 256, 384)
+        quantize(c_codes, c_scales, c_bf, 384, 512)
+        for g, t in early:
+            for q in range(2, 4):
+                score(g, t, q)
+        for g, t in [(1, 0), (2, 1), (3, 1), (2, 0), (3, 0)]:
+            for q in range(4):
+                score(g, t, q)
+
+        def col(g, t):
+            return neg_rt[:, g * HALVES + t : g * HALVES + t + 1]
+
+        def evacuate(g):
+            nc.scalar.activation(out=z1[g][:], in_=z[g][1][:], func=ACT.Copy, bias=1.0)
+            nc.gpsimd.tensor_tensor(out=diff[g][:, 1], in0=z1[g][:], in1=u_sb[g][:, 1], op=ALU.subtract)
+
+        def right_score(g, t):
+            nc.vector.scalar_tensor_tensor(
+                out=prod[g][:, t], in0=z[g][t][:], scalar=-1.0, in1=u_sb[g][:, t],
+                op0=ALU.mult, op1=ALU.mult, accum_out=col(g, t),
+            )
+
+        def margin(g, ns):
+            nc.vector.scalar_tensor_tensor(
+                out=diff[g][:, 0, ns], in0=z[g][0][:, ns], scalar=1.0, in1=u_sb[g][:, 0, ns],
+                op0=ALU.add, op1=ALU.subtract,
+            )
+
+        def hinge(g, t, ns):
+            nc.scalar.activation(out=y_sb[g][:, t, ns], in_=diff[g][:, t, ns], func=ACT.Relu, bias=col(g, t))
+
+        whole = slice(0, N)
+        evacuate(0)
+        evacuate(1)
+        evacuate(2)
+        for g in range(G - 1):
+            for t in (0, 1) if g == 0 else (1, 0):
+                right_score(g, t)
+            margin(g, whole)
+            hinge(g, 1, whole)
+            hinge(g, 0, whole)
+            nc.sync.dma_start(out=out_view[g], in_=y_sb[g][:])
+            if g == 0:
+                evacuate(3)
+        g = G - 1
+        right_score(g, 1)
+        hinge(g, 1, whole)
+        nc.sync.dma_start(out=out_view[g][:, 1], in_=y_sb[g][:, 1])
+        right_score(g, 0)
+        for ns in (slice(0, N // 2), slice(N // 2, N)):
+            margin(g, ns)
+            hinge(g, 0, ns)
+            nc.sync.dma_start(out=out_view[g][:, 0, ns], in_=y_sb[g][:, 0, ns])

@@ -18,14 +18,7 @@ PACK = 4
 ROWS = D // PACK
 HALVES = M // P
 NQ = 128
-C_LOAD = 256
-
-
-def interleave(copy, grouped, raw, lo, hi, base):
-    copy(
-        out=grouped[:, base + lo : base + hi, :].rearrange("p (c i) j -> p c j i", i=4),
-        in_=raw[:, :, lo:hi].rearrange("p j (c i) -> p c j i", i=4),
-    )
+HN = N // 2
 
 
 def tile_rows_hinge_kernel(tc, x, c, u, out):
@@ -35,32 +28,34 @@ def tile_rows_hinge_kernel(tc, x, c, u, out):
         ps = ctx.enter_context(tc.psum_pool(name="ps", bufs=1))
         ctx.enter_context(tc.manual_schedule())
 
-        x_raw = sb.tile([P, PACK, M], F32, name="x_raw")
-        c_raw = [sb.tile([P, PACK, C_LOAD], F32, name="c_raw%d" % h) for h in range(N // C_LOAD)]
-        u_sb = [sb.tile([P, HALVES, N], F32, name="u%d" % g) for g in range(G)]
-        y_sb = [sb.tile([P, HALVES, N], F32, name="y%d" % g) for g in range(G)]
-        diff = [sb.tile([P, HALVES, N], F32, name="diff%d" % g) for g in range(G)]
-        prod = [sb.tile([P, HALVES, N], F32, name="prod%d" % g) for g in range(G)]
-        z1 = [sb.tile([P, N], F32, name="z1_%d" % g) for g in range(G)]
-        neg_rt = sb.tile([P, G * HALVES], F32, name="neg_rt")
-        x_bf = sb.tile([P, HALVES, P, PACK], BF16, name="x_bf", align_bytes=64)
+        tiles = [(g, t) for t in range(HALVES) for g in range(G)]
+        x_raw = [sb.tile([P, PACK, P], F32, name="x_raw%d" % t) for t in range(HALVES)]
+        c_raw = [sb.tile([P, PACK, HN], F32, name="c_raw%d" % h) for h in range(2)]
+        u_sb = {k: sb.tile([P, N], F32, name="u%d_%d" % k) for k in tiles}
+        y_sb = {k: sb.tile([P, N], F32, name="y%d_%d" % k) for k in tiles}
+        diff = {k: sb.tile([P, N], F32, name="diff%d_%d" % k) for k in tiles}
+        prod = {k: sb.tile([P, N], F32, name="prod%d_%d" % k) for k in tiles}
+        z1 = {k: sb.tile([P, N], F32, name="z1_%d_%d" % k) for k in tiles if k[0] % 2}
+        z = {k: ps.tile([P, N], F32, name="z%d_%d" % k) for k in tiles}
+        neg_rt = sb.tile([P, len(tiles)], F32, name="neg_rt")
+        x_bf = sb.tile([P, M, PACK], BF16, name="x_bf", align_bytes=64)
         c_bf = sb.tile([P, N, PACK], BF16, name="c_bf", align_bytes=64)
         x_codes = sb.tile([P, M], U32, name="x_codes", align_bytes=64)
         x_scales = sb.tile([P, M], U8, name="x_scales", align_bytes=64)
         c_codes = sb.tile([P, N], U32, name="c_codes", align_bytes=64)
         c_scales = sb.tile([P, N], U8, name="c_scales", align_bytes=64)
-        z = [[ps.tile([P, N], F32, name="z%d_%d" % (g, t)) for t in range(HALVES)] for g in range(G)]
 
         x_view = x.rearrange("g (p j) m -> (g p) j m", j=PACK)
         c_view = c.rearrange("g (p j) n -> (g p) j n", j=PACK)
-        u_view = u.rearrange("g (s t) n -> g s t n", t=HALVES)
-        out_view = out.rearrange("g (s t) n -> g s t n", t=HALVES)
 
-        nc.sync.dma_start(out=x_raw[:], in_=x_view)
-        for h in range(N // C_LOAD):
-            nc.sync.dma_start(out=c_raw[h][:], in_=c_view[:, :, h * C_LOAD : (h + 1) * C_LOAD])
-        for g in range(G):
-            nc.sync.dma_start(out=u_sb[g][:], in_=u_view[g])
+        def scalar_cast(out, in_):
+            nc.scalar.activation(out=out, in_=in_, func=ACT.Copy)
+
+        def interleave(copy, grouped, raw, base, lo, hi):
+            copy(
+                out=grouped[:, base + lo : base + hi, :].rearrange("p (c i) j -> p c j i", i=4),
+                in_=raw[:, :, lo:hi].rearrange("p j (c i) -> p c j i", i=4),
+            )
 
         def quantize(codes, scales, grouped, lo, hi):
             nc.vector.quantize_mx(
@@ -69,86 +64,110 @@ def tile_rows_hinge_kernel(tc, x, c, u, out):
                 in_=grouped[:, lo:hi, :].rearrange("p n j -> p (n j)"),
             )
 
-        def score(g, t, q):
+        def score(k, quarters):
+            g, t = k
             rows = slice(g * ROWS, (g + 1) * ROWS)
             ms = slice(t * P, (t + 1) * P)
-            ns = slice(q * NQ, (q + 1) * NQ)
-            nc.tensor.matmul_mx(
-                out=z[g][t][:, ns],
-                lhsT=x_codes[rows, ms].bitcast(FP8X4),
-                lhsT_scale=x_scales[rows, ms],
-                rhs=c_codes[rows, ns].bitcast(FP8X4),
-                rhs_scale=c_scales[rows, ns],
-                start=True,
-                stop=True,
+            for q in quarters:
+                ns = slice(q * NQ, (q + 1) * NQ)
+                nc.tensor.matmul_mx(
+                    out=z[k][:, ns],
+                    lhsT=x_codes[rows, ms].bitcast(FP8X4),
+                    lhsT_scale=x_scales[rows, ms],
+                    rhs=c_codes[rows, ns].bitcast(FP8X4),
+                    rhs_scale=c_scales[rows, ns],
+                    start=True,
+                    stop=True,
+                )
+
+        def col(k):
+            i = tiles.index(k)
+            return neg_rt[:, i : i + 1]
+
+        def evacuate(k, ns):
+            nc.scalar.activation(out=z1[k][:, ns], in_=z[k][:, ns], func=ACT.Copy, bias=1.0)
+
+        def margin_pool(k):
+            nc.gpsimd.tensor_tensor(out=diff[k][:], in0=z1[k][:], in1=u_sb[k][:], op=ALU.subtract)
+
+        def right_score(k):
+            nc.vector.scalar_tensor_tensor(
+                out=prod[k][:], in0=z[k][:], scalar=-1.0, in1=u_sb[k][:],
+                op0=ALU.mult, op1=ALU.mult, accum_out=col(k),
             )
 
-        x_dealt = x_raw[:].rearrange("p j (s t) -> p t s j", t=HALVES)
-        nc.scalar.activation(out=x_bf[:, 1], in_=x_dealt[:, 1], func=ACT.Copy)
-        nc.vector.tensor_copy(out=x_bf[:, 0], in_=x_dealt[:, 0])
-        quantize(x_codes, x_scales, x_bf[:].rearrange("p t s j -> p (t s) j"), 0, M)
-
-        interleave(nc.vector.tensor_copy, c_bf, c_raw[0], 0, 160, 0)
-        interleave(nc.scalar.copy, c_bf, c_raw[0], 160, 256, 0)
-        quantize(c_codes, c_scales, c_bf, 0, 256)
-        early = [(0, 0), (0, 1), (1, 1)]
-        for g, t in early:
-            for q in range(2):
-                score(g, t, q)
-
-        interleave(nc.vector.tensor_copy, c_bf, c_raw[1], 0, 128, 256)
-        interleave(nc.scalar.copy, c_bf, c_raw[1], 128, 224, 256)
-        interleave(nc.vector.tensor_copy, c_bf, c_raw[1], 224, 256, 256)
-        quantize(c_codes, c_scales, c_bf, 256, 384)
-        quantize(c_codes, c_scales, c_bf, 384, 512)
-        for g, t in early:
-            for q in range(2, 4):
-                score(g, t, q)
-        for g, t in [(1, 0), (2, 1), (3, 1), (2, 0), (3, 0)]:
-            for q in range(4):
-                score(g, t, q)
-
-        def col(g, t):
-            return neg_rt[:, g * HALVES + t : g * HALVES + t + 1]
-
-        def evacuate(g):
-            nc.scalar.activation(out=z1[g][:], in_=z[g][1][:], func=ACT.Copy, bias=1.0)
-            nc.gpsimd.tensor_tensor(out=diff[g][:, 1], in0=z1[g][:], in1=u_sb[g][:, 1], op=ALU.subtract)
-
-        def right_score(g, t):
+        def margin(k, ns):
             nc.vector.scalar_tensor_tensor(
-                out=prod[g][:, t], in0=z[g][t][:], scalar=-1.0, in1=u_sb[g][:, t],
-                op0=ALU.mult, op1=ALU.mult, accum_out=col(g, t),
-            )
-
-        def margin(g, ns):
-            nc.vector.scalar_tensor_tensor(
-                out=diff[g][:, 0, ns], in0=z[g][0][:, ns], scalar=1.0, in1=u_sb[g][:, 0, ns],
+                out=diff[k][:, ns], in0=z[k][:, ns], scalar=1.0, in1=u_sb[k][:, ns],
                 op0=ALU.add, op1=ALU.subtract,
             )
 
-        def hinge(g, t, ns):
-            nc.scalar.activation(out=y_sb[g][:, t, ns], in_=diff[g][:, t, ns], func=ACT.Relu, bias=col(g, t))
+        def hinge(k, ns):
+            g, t = k
+            nc.scalar.activation(out=y_sb[k][:, ns], in_=diff[k][:, ns], func=ACT.Relu, bias=col(k))
+            nc.sync.dma_start(out=out[g, t * P : (t + 1) * P, ns], in_=y_sb[k][:, ns])
 
-        whole = slice(0, N)
-        evacuate(0)
-        evacuate(1)
-        evacuate(2)
-        for g in range(G - 1):
-            for t in (0, 1) if g == 0 else (1, 0):
-                right_score(g, t)
-            margin(g, whole)
-            hinge(g, 1, whole)
-            hinge(g, 0, whole)
-            nc.sync.dma_start(out=out_view[g], in_=y_sb[g][:])
-            if g == 0:
-                evacuate(3)
-        g = G - 1
-        right_score(g, 1)
-        hinge(g, 1, whole)
-        nc.sync.dma_start(out=out_view[g][:, 1], in_=y_sb[g][:, 1])
-        right_score(g, 0)
-        for ns in (slice(0, N // 2), slice(N // 2, N)):
-            margin(g, ns)
-            hinge(g, 0, ns)
-            nc.sync.dma_start(out=out_view[g][:, 0, ns], in_=y_sb[g][:, 0, ns])
+        v = tiles[0::2]
+        w = tiles[1::2]
+        whole, first, second = slice(0, N), slice(0, HN), slice(HN, N)
+
+        nc.sync.dma_start(out=x_raw[0][:], in_=x_view[:, :, 0:P])
+        for h in range(2):
+            nc.sync.dma_start(out=c_raw[h][:], in_=c_view[:, :, h * HN : (h + 1) * HN])
+        nc.sync.dma_start(out=x_raw[1][:], in_=x_view[:, :, P:M])
+        for g, t in [v[0], w[0], w[1], v[1], w[2], v[2], w[3], v[3]]:
+            nc.sync.dma_start(out=u_sb[g, t][:], in_=u[g, t * P : (t + 1) * P, :])
+
+        interleave(scalar_cast, x_bf, x_raw[0], 0, 80, 128)
+        interleave(nc.vector.tensor_copy, x_bf, x_raw[0], 0, 0, 80)
+        quantize(x_codes, x_scales, x_bf, 0, P)
+
+        interleave(nc.vector.tensor_copy, c_bf, c_raw[0], 0, 0, 160)
+        interleave(nc.scalar.copy, c_bf, c_raw[0], 0, 160, 256)
+        quantize(c_codes, c_scales, c_bf, 0, HN)
+        for k in (w[0], v[0], w[1]):
+            score(k, (0, 1))
+
+        interleave(nc.vector.tensor_copy, c_bf, c_raw[1], HN, 0, 128)
+        interleave(nc.scalar.copy, c_bf, c_raw[1], HN, 128, 224)
+        interleave(nc.vector.tensor_copy, c_bf, c_raw[1], HN, 224, 256)
+        quantize(c_codes, c_scales, c_bf, 256, 384)
+        quantize(c_codes, c_scales, c_bf, 384, 512)
+
+        evacuate(w[0], first)
+        interleave(nc.vector.tensor_copy, x_bf, x_raw[1], P, 0, 80)
+        interleave(nc.scalar.copy, x_bf, x_raw[1], P, 80, 128)
+        quantize(x_codes, x_scales, x_bf, P, M)
+        evacuate(w[1], first)
+
+        for k in (v[0], w[0], w[1]):
+            score(k, (2, 3))
+        for k in (w[2], v[1], w[3], v[2], v[3]):
+            score(k, range(4))
+
+        evacuate(w[0], second)
+        margin_pool(w[0])
+        evacuate(w[1], second)
+        margin_pool(w[1])
+        evacuate(w[2], whole)
+        margin_pool(w[2])
+
+        right_score(v[0])
+        right_score(w[0])
+        margin(v[0], whole)
+        hinge(v[0], whole)
+        hinge(w[0], whole)
+        evacuate(w[3], whole)
+        margin_pool(w[3])
+        for i in (1, 2):
+            right_score(w[i])
+            right_score(v[i])
+            margin(v[i], whole)
+            hinge(w[i], whole)
+            hinge(v[i], whole)
+        right_score(w[3])
+        hinge(w[3], whole)
+        right_score(v[3])
+        for ns in (first, second):
+            margin(v[3], ns)
+            hinge(v[3], ns)

@@ -31,8 +31,10 @@ def tile_rows_hinge_kernel(tc, x, c, u, out):
         tiles = [(g, t) for t in range(HALVES) for g in range(G)]
         x_raw = [sb.tile([P, PACK, P], F32, name="x_raw%d" % t) for t in range(HALVES)]
         c_raw = [sb.tile([P, PACK, HN], F32, name="c_raw%d" % h) for h in range(2)]
-        u_sb = {k: sb.tile([P, N], F32, name="u%d_%d" % k) for k in tiles}
-        y_sb = {k: sb.tile([P, N], F32, name="y%d_%d" % k) for k in tiles}
+        u_pair = [sb.tile([P, 2, N], F32, name="u%d" % i) for i in range(4)]
+        u_sb = {k: u_pair[i // 2][:, i % 2] for i, k in enumerate(tiles)}
+        y_pair = [sb.tile([P, 2, N], F32, name="y%d" % i) for i in range(4)]
+        y_sb = {k: y_pair[i // 2][:, i % 2] for i, k in enumerate(tiles)}
         diff = {k: sb.tile([P, N], F32, name="diff%d_%d" % k) for k in tiles}
         prod = {k: sb.tile([P, N], F32, name="prod%d_%d" % k) for k in tiles}
         z1 = {k: sb.tile([P, N], F32, name="z1_%d_%d" % k) for k in tiles if k[0] % 2}
@@ -88,11 +90,11 @@ def tile_rows_hinge_kernel(tc, x, c, u, out):
             nc.scalar.activation(out=z1[k][:, ns], in_=z[k][:, ns], func=ACT.Copy, bias=1.0)
 
         def margin_pool(k):
-            nc.gpsimd.tensor_tensor(out=diff[k][:], in0=z1[k][:], in1=u_sb[k][:], op=ALU.subtract)
+            nc.gpsimd.tensor_tensor(out=diff[k][:], in0=z1[k][:], in1=u_sb[k], op=ALU.subtract)
 
         def right_score(k):
             nc.vector.scalar_tensor_tensor(
-                out=prod[k][:], in0=z[k][:], scalar=-1.0, in1=u_sb[k][:],
+                out=prod[k][:], in0=z[k][:], scalar=-1.0, in1=u_sb[k],
                 op0=ALU.mult, op1=ALU.mult, accum_out=col(k),
             )
 
@@ -102,9 +104,16 @@ def tile_rows_hinge_kernel(tc, x, c, u, out):
                 op0=ALU.add, op1=ALU.subtract,
             )
 
+        def pair_view(a, i):
+            g, t = tiles[2 * i]
+            return a[g : g + 2, t * P : (t + 1) * P, :].rearrange("g s n -> s g n")
+
+        def hinge_only(k, ns):
+            nc.scalar.activation(out=y_sb[k][:, ns], in_=diff[k][:, ns], func=ACT.Relu, bias=col(k))
+
         def hinge(k, ns):
             g, t = k
-            nc.scalar.activation(out=y_sb[k][:, ns], in_=diff[k][:, ns], func=ACT.Relu, bias=col(k))
+            hinge_only(k, ns)
             nc.sync.dma_start(out=out[g, t * P : (t + 1) * P, ns], in_=y_sb[k][:, ns])
 
         v = tiles[0::2]
@@ -115,8 +124,10 @@ def tile_rows_hinge_kernel(tc, x, c, u, out):
         for h in range(2):
             nc.sync.dma_start(out=c_raw[h][:], in_=c_view[:, :, h * HN : (h + 1) * HN])
         nc.sync.dma_start(out=x_raw[1][:], in_=x_view[:, :, P:M])
-        for g, t in [v[0], w[0], w[1], v[1], w[2], v[2], w[3], v[3]]:
-            nc.sync.dma_start(out=u_sb[g, t][:], in_=u[g, t * P : (t + 1) * P, :])
+        for g, t in (v[0], w[0]):
+            nc.sync.dma_start(out=u_sb[g, t], in_=u[g, t * P : (t + 1) * P, :])
+        for i in range(1, 4):
+            nc.sync.dma_start(out=u_pair[i][:], in_=pair_view(u, i))
 
         interleave(scalar_cast, x_bf, x_raw[0], 0, 80, 128)
         interleave(nc.vector.tensor_copy, x_bf, x_raw[0], 0, 0, 80)

from contextlib import ExitStack

import concourse.mybir as mybir

G, D, M, N = 4, 128, 256, 512
FLOPS = 2 * G * D * M * N

F32 = mybir.dt.float32
BF16 = mybir.dt.bfloat16
U32 = mybir.dt.uint32
U8 = mybir.dt.uint8
FP8X4 = mybir.dt.float8_e4m3fn_x4
ALU = mybir.AluOpType
ACT = mybir.ActivationFunctionType

P = 128
PACK = 4
ROWS = D // PACK
HALVES = M // P
NQ = 128
HN = N // 2


def tile_rows_hinge_kernel(tc, x, c, u, out):
    nc = tc.nc
    with ExitStack() as ctx:
        sb = ctx.enter_context(tc.tile_pool(name="sb", bufs=1))
        ps = ctx.enter_context(tc.psum_pool(name="ps", bufs=1))
        ctx.enter_context(tc.manual_schedule())

        tiles = [(g, t) for t in range(HALVES) for g in range(G)]
        x_raw = [sb.tile([P, PACK, P], F32, name="x_raw%d" % t) for t in range(HALVES)]
        c_raw = [sb.tile([P, PACK, HN], F32, name="c_raw%d" % h) for h in range(2)]
        u_pair = [sb.tile([P, 2, N], F32, name="u%d" % i) for i in range(4)]
        u_sb = {k: u_pair[i // 2][:, i % 2] for i, k in enumerate(tiles)}
        y_pair = [sb.tile([P, 2, N], F32, name="y%d" % i) for i in range(4)]
        y_sb = {k: y_pair[i // 2][:, i % 2] for i, k in enumerate(tiles)}
        diff = {k: sb.tile([P, N], F32, name="diff%d_%d" % k) for k in tiles}
        prod = {k: sb.tile([P, N], F32, name="prod%d_%d" % k) for k in tiles}
        z1 = {k: sb.tile([P, N], F32, name="z1_%d_%d" % k) for k in tiles if k[0] % 2}
        z = {k: ps.tile([P, N], F32, name="z%d_%d" % k) for k in tiles}
        neg_rt = sb.tile([P, len(tiles)], F32, name="neg_rt")
        x_bf = sb.tile([P, M, PACK], BF16, name="x_bf", align_bytes=64)
        c_bf = sb.tile([P, N, PACK], BF16, name="c_bf", align_bytes=64)
        x_codes = sb.tile([P, M], U32, name="x_codes", align_bytes=64)
        x_scales = sb.tile([P, M], U8, name="x_scales", align_bytes=64)
        c_codes = sb.tile([P, N], U32, name="c_codes", align_bytes=64)
        c_scales = sb.tile([P, N], U8, name="c_scales", align_bytes=64)

        x_view = x.rearrange("g (p j) m -> (g p) j m", j=PACK)
        c_view = c.rearrange("g (p j) n -> (g p) j n", j=PACK)

        def scalar_cast(out, in_):
            nc.scalar.activation(out=out, in_=in_, func=ACT.Copy)

        def interleave(copy, grouped, raw, base, lo, hi):
            copy(
                out=grouped[:, base + lo : base + hi, :].rearrange("p (c i) j -> p c j i", i=4),
                in_=raw[:, :, lo:hi].rearrange("p j (c i) -> p c j i", i=4),
            )

        def quantize(codes, scales, grouped, lo, hi):
            nc.vector.quantize_mx(
                out=codes[:, lo:hi].bitcast(FP8X4),
                scales=scales[:, lo:hi],
                in_=grouped[:, lo:hi, :].rearrange("p n j -> p (n j)"),
            )

        def score(k, quarters):
            g, t = k
            rows = slice(g * ROWS, (g + 1) * ROWS)
            ms = slice(t * P, (t + 1) * P)
            for q in quarters:
                ns = slice(q * NQ, (q + 1) * NQ)
                nc.tensor.matmul_mx(
                    out=z[k][:, ns],
                    lhsT=x_codes[rows, ms].bitcast(FP8X4),
                    lhsT_scale=x_scales[rows, ms],
                    rhs=c_codes[rows, ns].bitcast(FP8X4),
                    rhs_scale=c_scales[rows, ns],
                    start=True,
                    stop=True,
                )

        def col(k):
            i = tiles.index(k)
            return neg_rt[:, i : i + 1]

        def evacuate(k, ns):
            nc.scalar.activation(out=z1[k][:, ns], in_=z[k][:, ns], func=ACT.Copy, bias=1.0)

        def margin_pool(k):
            nc.gpsimd.tensor_tensor(out=diff[k][:], in0=z1[k][:], in1=u_sb[k], op=ALU.subtract)

        def right_score(k):
            nc.vector.scalar_tensor_tensor(
                out=prod[k][:], in0=z[k][:], scalar=-1.0, in1=u_sb[k],
                op0=ALU.mult, op1=ALU.mult, accum_out=col(k),
            )

        def margin(k, ns):
            nc.vector.scalar_tensor_tensor(
                out=diff[k][:, ns], in0=z[k][:, ns], scalar=1.0, in1=u_sb[k][:, ns],
                op0=ALU.add, op1=ALU.subtract,
            )

        def pair_view(a, i):
            g, t = tiles[2 * i]
            return a[g : g + 2, t * P : (t + 1) * P, :].rearrange("g s n -> s g n")

        def hinge_only(k, ns):
            nc.scalar.activation(out=y_sb[k][:, ns], in_=diff[k][:, ns], func=ACT.Relu, bias=col(k))

        def hinge(k, ns):
            g, t = k
            hinge_only(k, ns)
            nc.sync.dma_start(out=out[g, t * P : (t + 1) * P, ns], in_=y_sb[k][:, ns])

        v = tiles[0::2]
        w = tiles[1::2]
        whole, first, second = slice(0, N), slice(0, HN), slice(HN, N)

        nc.sync.dma_start(out=x_raw[0][:], in_=x_view[:, :, 0:P])
        for h in range(2):
            nc.sync.dma_start(out=c_raw[h][:], in_=c_view[:, :, h * HN : (h + 1) * HN])
        nc.sync.dma_start(out=x_raw[1][:], in_=x_view[:, :, P:M])
        for g, t in (v[0], w[0]):
            nc.sync.dma_start(out=u_sb[g, t], in_=u[g, t * P : (t + 1) * P, :])
        for i in range(1, 4):
            nc.sync.dma_start(out=u_pair[i][:], in_=pair_view(u, i))

        interleave(scalar_cast, x_bf, x_raw[0], 0, 80, 128)
        interleave(nc.vector.tensor_copy, x_bf, x_raw[0], 0, 0, 80)
        quantize(x_codes, x_scales, x_bf, 0, P)

        interleave(nc.vector.tensor_copy, c_bf, c_raw[0], 0, 0, 160)
        interleave(nc.scalar.copy, c_bf, c_raw[0], 0, 160, 256)
        quantize(c_codes, c_scales, c_bf, 0, HN)
        for k in (w[0], v[0], w[1]):
            score(k, (0, 1))

        interleave(nc.vector.tensor_copy, c_bf, c_raw[1], HN, 0, 128)
        interleave(nc.scalar.copy, c_bf, c_raw[1], HN, 128, 224)
        interleave(nc.vector.tensor_copy, c_bf, c_raw[1], HN, 224, 256)
        quantize(c_codes, c_scales, c_bf, 256, 384)
        quantize(c_codes, c_scales, c_bf, 384, 512)

        evacuate(w[0], first)
        interleave(nc.vector.tensor_copy, x_bf, x_raw[1], P, 0, 80)
        interleave(nc.scalar.copy, x_bf, x_raw[1], P, 80, 128)
        quantize(x_codes, x_scales, x_bf, P, M)
        evacuate(w[1], first)

        for k in (v[0], w[0], w[1]):
            score(k, (2, 3))
        for k in (w[2], v[1], w[3], v[2], v[3]):
            score(k, range(4))

        evacuate(w[0], second)
        margin_pool(w[0])
        evacuate(w[1], second)
        margin_pool(w[1])
        evacuate(w[2], whole)
        margin_pool(w[2])

        right_score(v[0])
        right_score(w[0])
        margin(v[0], whole)
        hinge(v[0], whole)
        hinge(w[0], whole)
        evacuate(w[3], whole)
        margin_pool(w[3])
        for i in (1, 2):
            right_score(w[i])
            right_score(v[i])
            margin(v[i], whole)
            hinge(w[i], whole)
            hinge(v[i], whole)
        right_score(w[3])
        hinge(w[3], whole)
        right_score(v[3])
        for ns in (first, second):
            margin(v[3], ns)
            hinge(v[3], ns)
